import numpy as np
import ml_dtypes

BF16 = ml_dtypes.bfloat16


def bf(x):
    return np.asarray(x, np.float32).astype(BF16)


def f32(x):
    return np.asarray(x, np.float32)


def f64(x):
    return np.asarray(x).astype(np.float64)


def striped(idx):
    return np.tile(idx.reshape(-1, 16).T, (8, 1))


S, K, M, N, B, Q = 512, 128, 256, 128, 2, 64


def setup_inputs():
    return {"base": bf(np.random.standard_normal((B, M, S))), "x": bf(np.random.standard_normal((K, N))), "w": bf(np.random.standard_normal((K, M)) / np.sqrt(K)), "s": f32(0.5 + np.random.random_sample((M, 1))), "b": f32(0.5 * np.random.standard_normal((M, 1))), "offs": striped(np.random.permutation(S)[:N])}


def reference(base, x, w, s, b, offs):
    idx = offs[:16].T.reshape(-1)
    z = f64(base).copy()
    for i in range(B):
        z[i][:, idx[i * Q : (i + 1) * Q]] = f64(w).T @ f64(x)[:, i * Q : (i + 1) * Q]
    return z * f64(s) + f64(b)

@@ -1,0 +1,71 @@
+import concourse.mybir as mybir
+from concourse.masks import make_identity
+
+BF16, F32, U16 = mybir.dt.bfloat16, mybir.dt.float32, mybir.dt.uint16
+IDENTITY = mybir.ActivationFunctionType.Identity
+MULT, ADD = mybir.AluOpType.mult, mybir.AluOpType.add
+
+P = 128
+K, M, N = 128, 256, 128
+SEQS, TOKENS = 2, 512
+BLOCKS = M // P
+Q = N // SEQS
+OFFSETS_PER_COLUMN = 16
+
+FLOPS = 2 * K * M * N
+
+
+def tile_scatter_matmul_kernel(tc, base, x, w, s, b, offs, out):
+    nc = tc.nc
+    with tc.tile_pool(name="held", bufs=1) as held, tc.psum_pool(name="psum", bufs=1) as psum:
+        base_tiles = []
+        for i in range(SEQS):
+            base_tile = held.tile([P, BLOCKS, TOKENS], BF16, name=f"base{i}")
+            nc.sync.dma_start(base_tile[:], base[i].rearrange("(h p) t -> p h t", p=P))
+            base_tiles.append(base_tile)
+        offsets = held.tile([P, N // OFFSETS_PER_COLUMN], U16, name="offsets")
+        nc.sync.dma_start(offsets[:], offs)
+
+        weights = held.tile([K, M], BF16, name="weights")
+        nc.scalar.dma_start(weights[:], w)
+        moving = held.tile([K, N], BF16, name="moving")
+        nc.scalar.dma_start(moving[:], x)
+        gain = held.tile([P, BLOCKS], F32, name="gain")
+        nc.scalar.dma_start(gain[:], s.rearrange("(h p) o -> p (h o)", p=P))
+        shift = held.tile([P, BLOCKS], F32, name="shift")
+        nc.scalar.dma_start(shift[:], b.rearrange("(h p) o -> p (h o)", p=P))
+
+        ident = held.tile([P, P], BF16, name="ident")
+        make_identity(nc, ident[:])
+
+        window_of = {}
+        for i in range(SEQS):
+            for h in range(BLOCKS):
+                window = psum.tile([P, TOKENS], F32, name=f"window{i}{h}")
+                nc.tensor.matmul(window[:], ident[:], base_tiles[i][:, h, :], start=True, stop=True)
+                window_of[i, h] = window
+
+        piece = Q // OFFSETS_PER_COLUMN
+        for i in range(SEQS):
+            for h in range(BLOCKS):
+                nc.tensor.matmul(
+                    window_of[i, h][:].indirect(offsets[:, i * piece : (i + 1) * piece]),
+                    weights[:, h * P : (h + 1) * P],
+                    moving[:, i * Q : (i + 1) * Q],
+                    start=True,
+                    stop=True,
+                )
+
+        for i in range(SEQS):
+            for h in range(BLOCKS):
+                result = held.tile([P, TOKENS], F32, name=f"result{i}{h}")
+                if h == 0:
+                    nc.vector.tensor_scalar(
+                        result[:], window_of[i, h][:], gain[:, h : h + 1], shift[:, h : h + 1], op0=MULT, op1=ADD
+                    )
+                    nc.sync.dma_start(out[i, h * P : (h + 1) * P, :], result[:])
+                else:
+                    nc.scalar.activation(
+                        result[:], window_of[i, h][:], IDENTITY, bias=shift[:, h : h + 1], scale=gain[:, h : h + 1]
+                    )
+                    nc.scalar.dma_start(out[i, h * P : (h + 1) * P, :], result[:])

@@ -12,6 +12,8 @@ BLOCKS = M // P
 Q = N // SEQS
 OFFSETS_PER_COLUMN = 16
 
+WARM_UPS = 4
+
 FLOPS = 2 * K * M * N
 
 
@@ -37,6 +39,12 @@ def tile_scatter_matmul_kernel(tc, base, x, w, s, b, offs, out):
 
         ident = held.tile([P, P], BF16, name="ident")
         make_identity(nc, ident[:])
+
+        zeros = held.tile([P, TOKENS], BF16, name="zeros")
+        nc.vector.memset(zeros[:], 0.0)
+        spare = psum.tile([P, TOKENS], F32, name="spare")
+        for warm_up in range(WARM_UPS):
+            nc.tensor.matmul(spare[:], zeros[:, :P], zeros[:], start=True, stop=True)
 
         window_of = {}
         for i in range(SEQS):

@@ -46,6 +46,9 @@ def tile_scatter_matmul_kernel(tc, base, x, w, s, b, offs, out):
         for warm_up in range(WARM_UPS):
             nc.tensor.matmul(spare[:], zeros[:, :P], zeros[:], start=True, stop=True)
 
+        table_loaded = held.tile([P, 1], F32, name="table_loaded")
+        nc.scalar.activation(table_loaded[:], zeros[:, :1], IDENTITY)
+
         window_of = {}
         for i in range(SEQS):
             for h in range(BLOCKS):

@@ -12,7 +12,7 @@ BLOCKS = M // P
 Q = N // SEQS
 OFFSETS_PER_COLUMN = 16
 
-WARM_UPS = 4
+WARM_UPS = 3
 
 FLOPS = 2 * K * M * N
 
@@ -27,15 +27,15 @@ def tile_scatter_matmul_kernel(tc, base, x, w, s, b, offs, out):
             base_tiles.append(base_tile)
         offsets = held.tile([P, N // OFFSETS_PER_COLUMN], U16, name="offsets")
         nc.sync.dma_start(offsets[:], offs)
+        gain = held.tile([P, BLOCKS], F32, name="gain")
+        nc.sync.dma_start(gain[:], s.rearrange("(h p) o -> p (h o)", p=P))
+        shift = held.tile([P, BLOCKS], F32, name="shift")
+        nc.sync.dma_start(shift[:], b.rearrange("(h p) o -> p (h o)", p=P))
 
         weights = held.tile([K, M], BF16, name="weights")
         nc.scalar.dma_start(weights[:], w)
         moving = held.tile([K, N], BF16, name="moving")
         nc.scalar.dma_start(moving[:], x)
-        gain = held.tile([P, BLOCKS], F32, name="gain")
-        nc.scalar.dma_start(gain[:], s.rearrange("(h p) o -> p (h o)", p=P))
-        shift = held.tile([P, BLOCKS], F32, name="shift")
-        nc.scalar.dma_start(shift[:], b.rearrange("(h p) o -> p (h o)", p=P))
 
         ident = held.tile([P, P], BF16, name="ident")
         make_identity(nc, ident[:])
@@ -67,16 +67,20 @@ def tile_scatter_matmul_kernel(tc, base, x, w, s, b, offs, out):
                     stop=True,
                 )
 
+        half = TOKENS // 2
         for i in range(SEQS):
             for h in range(BLOCKS):
-                result = held.tile([P, TOKENS], F32, name=f"result{i}{h}")
-                if h == 0:
-                    nc.vector.tensor_scalar(
-                        result[:], window_of[i, h][:], gain[:, h : h + 1], shift[:, h : h + 1], op0=MULT, op1=ADD
-                    )
-                    nc.sync.dma_start(out[i, h * P : (h + 1) * P, :], result[:])
-                else:
-                    nc.scalar.activation(
-                        result[:], window_of[i, h][:], IDENTITY, bias=shift[:, h : h + 1], scale=gain[:, h : h + 1]
-                    )
-                    nc.scalar.dma_start(out[i, h * P : (h + 1) * P, :], result[:])
+                for a in range(0, TOKENS, half):
+                    result = held.tile([P, half], F32, name=f"result{i}{h}{a}")
+                    placed = window_of[i, h][:, a : a + half]
+                    target = out[i, h * P : (h + 1) * P, a : a + half]
+                    if h == 0:
+                        nc.vector.tensor_scalar(
+                            result[:], placed, gain[:, h : h + 1], shift[:, h : h + 1], op0=MULT, op1=ADD
+                        )
+                        nc.sync.dma_start(target, result[:])
+                    else:
+                        nc.scalar.activation(
+                            result[:], placed, IDENTITY, bias=shift[:, h : h + 1], scale=gain[:, h : h + 1]
+                        )
+                        nc.scalar.dma_start(target, result[:])

@@ -12,7 +12,7 @@ BLOCKS = M // P
 Q = N // SEQS
 OFFSETS_PER_COLUMN = 16
 
-WARM_UPS = 3
+WARM_UPS = 16
 
 FLOPS = 2 * K * M * N
 
@@ -37,14 +37,14 @@ def tile_scatter_matmul_kernel(tc, base, x, w, s, b, offs, out):
         moving = held.tile([K, N], BF16, name="moving")
         nc.scalar.dma_start(moving[:], x)
 
+        zeros = held.tile([P, P], BF16, name="zeros")
+        nc.gpsimd.memset(zeros[:], 0.0)
+        spare = psum.tile([P, P], F32, name="spare")
+        for warm_up in range(WARM_UPS):
+            nc.tensor.matmul(spare[:], zeros[:], zeros[:], start=True, stop=True)
+
         ident = held.tile([P, P], BF16, name="ident")
         make_identity(nc, ident[:])
-
-        zeros = held.tile([P, TOKENS], BF16, name="zeros")
-        nc.vector.memset(zeros[:], 0.0)
-        spare = psum.tile([P, TOKENS], F32, name="spare")
-        for warm_up in range(WARM_UPS):
-            nc.tensor.matmul(spare[:], zeros[:, :P], zeros[:], start=True, stop=True)
 
         table_loaded = held.tile([P, 1], F32, name="table_loaded")
         nc.scalar.activation(table_loaded[:], zeros[:, :1], IDENTITY)

import concourse.mybir as mybir
from concourse.masks import make_identity

BF16, F32, U16 = mybir.dt.bfloat16, mybir.dt.float32, mybir.dt.uint16
IDENTITY = mybir.ActivationFunctionType.Identity
MULT, ADD = mybir.AluOpType.mult, mybir.AluOpType.add

P = 128
K, M, N = 128, 256, 128
SEQS, TOKENS = 2, 512
BLOCKS = M // P
Q = N // SEQS
OFFSETS_PER_COLUMN = 16

WARM_UPS = 16

FLOPS = 2 * K * M * N


def tile_scatter_matmul_kernel(tc, base, x, w, s, b, offs, out):
    nc = tc.nc
    with tc.tile_pool(name="held", bufs=1) as held, tc.psum_pool(name="psum", bufs=1) as psum:
        base_tiles = []
        for i in range(SEQS):
            base_tile = held.tile([P, BLOCKS, TOKENS], BF16, name=f"base{i}")
            nc.sync.dma_start(base_tile[:], base[i].rearrange("(h p) t -> p h t", p=P))
            base_tiles.append(base_tile)
        offsets = held.tile([P, N // OFFSETS_PER_COLUMN], U16, name="offsets")
        nc.sync.dma_start(offsets[:], offs)
        gain = held.tile([P, BLOCKS], F32, name="gain")
        nc.sync.dma_start(gain[:], s.rearrange("(h p) o -> p (h o)", p=P))
        shift = held.tile([P, BLOCKS], F32, name="shift")
        nc.sync.dma_start(shift[:], b.rearrange("(h p) o -> p (h o)", p=P))

        weights = held.tile([K, M], BF16, name="weights")
        nc.scalar.dma_start(weights[:], w)
        moving = held.tile([K, N], BF16, name="moving")
        nc.scalar.dma_start(moving[:], x)

        zeros = held.tile([P, P], BF16, name="zeros")
        nc.gpsimd.memset(zeros[:], 0.0)
        spare = psum.tile([P, P], F32, name="spare")
        for warm_up in range(WARM_UPS):
            nc.tensor.matmul(spare[:], zeros[:], zeros[:], start=True, stop=True)

        ident = held.tile([P, P], BF16, name="ident")
        make_identity(nc, ident[:])

        table_loaded = held.tile([P, 1], F32, name="table_loaded")
        nc.scalar.activation(table_loaded[:], zeros[:, :1], IDENTITY)

        window_of = {}
        for i in range(SEQS):
            for h in range(BLOCKS):
                window = psum.tile([P, TOKENS], F32, name=f"window{i}{h}")
                nc.tensor.matmul(window[:], ident[:], base_tiles[i][:, h, :], start=True, stop=True)
                window_of[i, h] = window

        piece = Q // OFFSETS_PER_COLUMN
        for i in range(SEQS):
            for h in range(BLOCKS):
                nc.tensor.matmul(
                    window_of[i, h][:].indirect(offsets[:, i * piece : (i + 1) * piece]),
                    weights[:, h * P : (h + 1) * P],
                    moving[:, i * Q : (i + 1) * Q],
                    start=True,
                    stop=True,
                )

        half = TOKENS // 2
        for i in range(SEQS):
            for h in range(BLOCKS):
                for a in range(0, TOKENS, half):
                    result = held.tile([P, half], F32, name=f"result{i}{h}{a}")
                    placed = window_of[i, h][:, a : a + half]
                    target = out[i, h * P : (h + 1) * P, a : a + half]
                    if h == 0:
                        nc.vector.tensor_scalar(
                            result[:], placed, gain[:, h : h + 1], shift[:, h : h + 1], op0=MULT, op1=ADD
                        )
                        nc.sync.dma_start(target, result[:])
                    else:
                        nc.scalar.activation(
                            result[:], placed, IDENTITY, bias=shift[:, h : h + 1], scale=gain[:, h : h + 1]
                        )
                        nc.scalar.dma_start(target, result[:])
